import numpy as np
CORES = [0,1,2,3]
N = 4
def setup_inputs(rng):
    return {"x": rng.standard_normal((N, 128, 4096), dtype=np.float32)}
def reference(x):
    s = np.maximum.accumulate(x, axis=0)
    return {"y": s.astype(x.dtype)}

from concourse.bass import DstId, RemoteDMATransfer

W = 4096
HELPERS = [4, 5, 6, 7]
NB = 4
BW = W // NB
MAX = 2

SCRATCH = {
    "xs": ("sbuf", [128, W], "float32"),
    "land": ("sbuf", [128, W], "float32"),
    "in0": ("sbuf", [128, BW], "float32"),
    "in1": ("sbuf", [128, BW], "float32"),
    "in2": ("sbuf", [128, BW], "float32"),
    "in3": ("sbuf", [128, BW], "float32"),
}
SEMAPHORES = (["sent", "stored"] + ["ld%d" % k for k in range(NB)] + ["res%d" % k for k in range(NB)]
              + ["a%d" % r for r in range(4)])


def helper_program(g, core, T, topo, k):
    blk = slice(k * BW, (k + 1) * BW)
    n = len(T.cores)
    g.wait_ge(T.sem.a0, 16)
    srcs = [T.in0[:]]
    for r in range(1, n):
        g.wait_ge(T.sem["a%d" % r], 16)
        srcs = srcs + [T["in%d" % r][:]]
        dst = T.cores[r]
        rid, pid, _se = topo.addr(dst)
        g.remote_dma_fused(
            [RemoteDMATransfer(dst_ids=[DstId(rid=rid, pnc=pid)], dma_engine_mask=topo.mask(core, dst),
                               remote_sem=T.sem["res%d" % k], srcs=srcs, dsts=[T.land[:, blk]], alu_op=MAX)],
            local_sem=T.sem.sent)
    g.wait_ge(T.sem.sent, 16 * (n - 1))


def rank_program(g, core, T, topo):
    rank = T.rank_of(core)
    if rank is None:
        if core in HELPERS:
            helper_program(g, core, T, topo, HELPERS.index(core))
        return

    blks = [slice(k * BW, (k + 1) * BW) for k in range(NB)]

    for k in range(NB):
        g.sync.dma_start(T.xs[:, blks[k]], T.x[:, blks[k]]).then_inc(T.sem["ld%d" % k], 16)

    if rank == 0:
        g.scalar.dma_start(T.y[:], T.x[:]).then_inc(T.sem.stored, 16)
        stores = 1
    else:
        for k in range(NB):
            g.scalar.wait_ge(T.sem["res%d" % k], 16)
            g.scalar.dma_start(T.y[:, blks[k]], T.land[:, blks[k]]).then_inc(T.sem.stored, 16)
        stores = NB

    for k in range(NB):
        dst = HELPERS[k]
        rid, pid, _se = topo.addr(dst)
        g.wait_ge(T.sem["ld%d" % k], 16)
        g.remote_dma(T["in%d" % rank][:], T.xs[:, blks[k]], T.sem["a%d" % rank], T.sem.sent,
                     pid, rid, topo.mask(core, dst))

    g.wait_ge(T.sem.sent, 16 * NB)
    g.wait_ge(T.sem.stored, 16 * stores)
